import numpy as np, ml_dtypes
CORES = [6,15,38,47]
N = 4
BF = ml_dtypes.bfloat16
def gentries(a):
    return np.ascontiguousarray(a.reshape(8, 16, -1).transpose(0, 2, 1)).reshape(8, -1)
def gtable(e):
    e = np.asarray(e); return np.ascontiguousarray(e.reshape(8, -1, 16).transpose(0, 2, 1)).reshape(128, -1).astype(np.int32)
S, B, T, RO = 3648, 32, 512, 3
H, TH, NC = S + 2 * RO * B, T // 2, (S + 2 * RO * B) // 16
G8 = np.arange(8)
def parts(rng, noise, skew):
    lab = np.argsort(rng.random((8, H)), axis=1).reshape(8, NC, 16); cl = np.zeros((8, H), np.int64)
    for g in range(8): cl[g, lab[g].reshape(-1)] = np.arange(H) // 16
    o = rng.integers(0, 16, (N, 8, 15, H))
    if skew: o = (o * rng.integers(0, 17, o.shape)) >> 4
    nm = lab[G8[None, :, None, None], ((cl + 1) % NC)[None, :, None, :], o]
    if noise > 0: nm = np.where(rng.random(nm.shape) < noise, rng.integers(0, H, nm.shape), nm)
    c = (rng.integers(0, NC, (1, 8, 1)) + np.arange(N)[:, None, None] * T + np.arange(T)[None, None, :]) % NC
    loose = lab[G8[None, :, None], c, rng.integers(0, 16, (N, 8, T))]; st = loose.copy()
    fol = rng.random((N, 8, T)) < 0.6; k = rng.integers(0, 15, (N, 8, T)); qn = np.arange(N)[:, None]
    for t in range(1, T): st[:, :, t] = np.where(fol[:, :, t], nm[qn, G8[None, :], k[:, :, t], st[:, :, t - 1]], loose[:, :, t])
    if noise > 0: st = np.where(rng.random(st.shape) < noise, rng.integers(0, H, st.shape), st)
    d = {"nm": nm, "wt": rng.integers(1, 256, (N, 8, 15, H)), "st": st}
    top = np.array([12, 60, 140, 255])[rng.integers(0, 4, (N, 8, 1))]
    d["w15"] = 1 + (top * rng.random((N, 8, H))).astype(np.int64)
    d["em"] = rng.integers(0, 16, (N, 8, 16, H)); d["ob"] = rng.integers(0, 16, (N, 8, 16, T)); d["xb"] = rng.integers(0, 16, (N, 8, 16))
    for n in ("a", "b", "v"): d[n] = rng.integers(0, 256, (N, 8, RO * T))
    return d, lab
def pack(d):
    lk = np.concatenate([256 * d["nm"] + d["wt"], d["w15"][:, :, None, :]], axis=2)
    return {"lk": np.ascontiguousarray(lk.reshape(N, 128, H)).astype(np.int32), "em": d["em"].reshape(N, 128, H).astype(np.float32).astype(BF),
            "ob": d["ob"].reshape(N, 128, T).astype(np.float32).astype(BF), "xb": d["xb"].reshape(N, 128, 1).astype(np.float32).astype(BF),
            "pe": np.stack([gtable(p[:, 0::2]) for p in d["st"]]), "po": np.stack([gtable(p[:, 1::2]) for p in d["st"]]),
            "nua": d["a"].astype(np.int32), "nub": d["b"].astype(np.int32), "vd": d["v"].astype(np.int32)}
def shares(t, n):
    return t // n + (np.arange(n) < t % n)
def tight(rng, d, g, i0):
    o = 2 + rng.permutation(S - 2)[:128]; X, Y, z = o[:8], o[8:].reshape(8, 15), o[8:]
    i = np.arange(i0, TH); p = np.arange(max(i0 - 1, 0), TH); vs = np.array([255, 255, 255, 255, 255, 255, 128, 128])
    x = d["st"][:, g]; x[:, 2 * p + 1] = X[p % 8]
    y = np.full(16, 15); y[15] = 1
    x = d["ob"][:, g]; x[:, :, 2 * i] = y[:, None]
    x = d["nm"][:, g]; x[:, :, X] = Y.T
    x[:, :8, z] = X[(np.arange(8)[:, None] + np.arange(120)[None, :]) % 8]; x[:, 8:, z] = rng.integers(0, H, (N, 7, 120))
    d["xb"][:, g] = 0
    for h in range(0, 2 * RO, 2):
        for n in ("a", "b"):
            x = d[n][:, g]; x[:, h * TH + i] = 0
        x = d["v"][:, g]; x[:, h * TH + i] = vs[(i - 1) % 8]
    for r in range(N):
        m = [int(rng.integers(17, 27)), int(rng.integers(33, 40)), int(rng.integers(65, 67)), int(rng.integers(180, 186)), int(rng.choice(np.array([7, 13, 14, 26, 28]))), int(rng.choice(np.array([52, 56, 104, 112])))]
        c6 = 128 * int(rng.integers(130, 181)) + int(rng.integers(1, 64)); c7 = 128 * int(rng.integers(130, 180)) + 65 + int(rng.integers(0, 64))
        case = ((1, 255 * m[0] + 1, m[0]), (2, 255 * m[1] + 1, m[1]), (4, 255 * m[2] + 1, m[2]), (13, 255 * m[3] + 1, m[3]),
                (3, 255 * m[4], m[4]), (9, 255 * m[5], m[5]),
                (7, c6, c6), (7, c7, c7 - 1))
        for j in range(8):
            k, c, rest = case[j]
            e = np.concatenate([shares(c, k + 1), shares(rest, 14 - k)]); a = e // 15
            F = np.zeros((16, 15), np.int64)
            F[:15] = (a // 15 + (np.arange(15)[:, None] < a % 15))[rng.permutation(15)]; F[15] = e - 15 * a
            x = d["em"][r, g]; x[:, Y[j]] = F
def setup_inputs(rng):
    return pack(parts(rng, 0.05, False)[0])
def setup_inputs_spread(rng):
    d, lab = parts(rng, 0.05, True)
    d["wt"] = np.minimum(np.exp2(8 * rng.random((N, 8, 15, H))).astype(np.int64), 255); d["w15"] = np.minimum(np.exp2(8 * rng.random((N, 8, H))).astype(np.int64), 255)
    top = np.array([2, 4, 8, 16])
    d["em"] = (top[rng.integers(0, 4, (N, 8, 1, H))] * rng.random((N, 8, 16, H))).astype(np.int64)
    d["ob"] = (top[rng.integers(0, 4, (N, 8, 1, T))] * rng.random((N, 8, 16, T))).astype(np.int64)
    d["a"] = (256 * rng.random(d["a"].shape) ** 2).astype(np.int64); d["b"] = (256 * rng.random(d["b"].shape) ** 3).astype(np.int64)
    d["v"] = np.where(rng.random(d["v"].shape) < 0.5, (256 * rng.random(d["v"].shape) ** 3).astype(np.int64), 255 - (256 * rng.random(d["v"].shape) ** 3).astype(np.int64))
    return pack(d)
def setup_inputs_ends(rng):
    d, lab = parts(rng, 0.0, False)
    m = rng.random(d["nm"].shape) < 0.76; hi = rng.random(d["nm"].shape) < 0.5
    d["nm"] = np.where(m, np.where(hi, H - 1, 0), d["nm"]); d["wt"] = np.where(hi, 255, 1)
    d["w15"] = 1 + 254 * rng.integers(0, 2, (N, 8, H))
    for n in ("em", "ob", "xb"): d[n] = 15 * rng.integers(0, 2, d[n].shape)
    d["st"] = np.where(rng.random(d["st"].shape) < 0.72, (H - 1) * rng.integers(0, 2, d["st"].shape), d["st"])
    for n in ("a", "b"): d[n] = 255 * rng.integers(0, 2, d[n].shape)
    v = 255 * rng.integers(0, 2, d["v"].shape)
    d["v"] = np.where(rng.random(v.shape) < 0.78, v, rng.choice(np.array([1, 127, 128, 129, 254]), v.shape))
    d["v"][:, 7] = np.where(rng.random((N, RO * T)) < 0.4, 128, d["v"][:, 7])
    ring = np.array([H - 1, 1, H - 1, H - 2, H - 1, 1, H - 1, H - 1, H - 2, H - 1, 1, H - 1, H - 2, H - 1, H - 2])
    for c, full in ((H - 1, 15), (H - 2, 9), (1, 11)):
        d["nm"][:, 7, :, c] = ring; d["wt"][:, 7, :, c] = np.where(np.arange(15) < full, 255, 1); d["w15"][:, 7, c] = 255; d["em"][:, 7, :, c] = 15
    d["nm"][:, 7, :, 0] = 0; d["wt"][:, 7, :, 0] = 1; d["w15"][:, 7, 0] = 1; d["em"][:, 7, :, 0] = 0; d["xb"][:, 7] = 15
    d["st"][:, 7] = rng.choice(np.array([0, 0, 0, 0, H - 1, H - 1, H - 1, H - 1, H - 2, 1]), (N, T))
    d["st"][:, 7, T - 3] = H - 1; d["st"][:, 7, T - 2] = 0; d["st"][:, 7, T - 1] = H - 1; d["st"][:, 7, 0] = H - 1
    o = rng.random((N, 8, 1, T)); d["ob"] = np.where(o < 0.08, 0, d["ob"])
    d["ob"][:, 7] = np.where(o[:, 7] > 0.5, 15, d["ob"][:, 7]); d["ob"][:, 7, :, T - 2:] = 15
    for h in range(2 * RO):
        j = h * TH + TH - 1; d["a"][:, 7, j] = 0; d["b"][:, 7, j] = 0; d["v"][:, 7, j] = 128
    X, L, V = (int(c) for c in 2 + rng.permutation(S - 2)[:3]); few = np.array([0, 16, 17, 18, 255]); rk = np.arange(N)
    x = d["nm"][:, 6]; x[(x == L) | (x == V)] = 0
    d["nm"][:, 6, :, L] = V; d["nm"][:, 6, :, V] = 0; d["nm"][:, 6, 0, V] = X; d["wt"][:, 6, 0, V] = 254; d["em"][:, 6, 0::2, V] = 15
    d["nm"][:, 6, :, X] = X; d["wt"][:, 6, :, X] = 255; d["w15"][:, 6, X] = 254; d["em"][:, 6, 0::2, X] = 15; d["xb"][:, 6, 0] = 15
    x = d["st"][:, 6]; x[(x == L) | (x == V)] = 0
    d["st"][:, 6] = np.where(rng.random((N, T)) < 0.7, X, d["st"][:, 6])
    d["st"][:, 6, :3] = X; d["st"][:, 6, T - 2 * RO - 4:] = X; d["ob"][:, 6, 0, :2] = 15
    x = d["st"][:, 6]; x[:, [TH - 1, TH + 8]] = L; x[:, [TH, TH + 1, TH + 9, TH + 10]] = X
    x = d["ob"][:, 6]; x[:, :, [TH - 1, TH, TH + 1, TH + 8, TH + 9, TH + 10]] = 0
    for n in ("a", "b"): d[n][:, 6] = few[rng.integers(0, 5, (N, RO * T))]
    for h in range(2 * RO):
        i = h * TH; j = i + TH - 1
        d["b"][:, 6, i] = few[rng.integers(0, 3, N)]; d["v"][:, 6, i] = 0
        d["a"][:, 6, j] = 17 + (rk + h) % 2; d["b"][:, 6, j] = 17 + ((rk + h) >> 1) % 2
        j = i + TH // 2 + 4 * (h & 1); d["a"][:, 6, j] = 0; d["b"][:, 6, j] = 17
    tight(rng, d, 5, TH - 16)
    return pack(d)
def setup_inputs_corners(rng):
    d, lab = parts(rng, 0.0, False)
    few = np.array([1, 2, 127, 128, 129, 238, 239, 240, 254, 255])
    d["wt"] = few[rng.integers(0, 10, (N, 8, 15, H))]; d["w15"] = few[rng.integers(0, 9, (N, 8, H))]
    for n in ("a", "b"): d[n] = rng.choice(np.array([0, 1, 128, 254, 255]), d[n].shape)
    d["v"] = rng.choice(np.array([0, 1, 127, 128, 129, 254, 255]), d["v"].shape)
    d["xb"][:, :, 0] = np.maximum(d["xb"][:, :, 0], 1); d["ob"][:, :, 0] = np.maximum(d["ob"][:, :, 0], 1)
    for g in range(8):
        o = rng.permutation(H); low, odd, z0 = o[:24], o[24:24 + TH + 32], o[24 + TH + 32]
        d["nm"][:, g] = low[rng.integers(0, 24, (N, 15, H))]
        for r in range(N):
            p = d["st"][r, g]; p[0::2] = low[rng.integers(0, 24, TH)]; p[1::2] = rng.permutation(odd)[:TH]; p[T - 1] = z0
            c = (g + r) % 8; n = (0, 1, B - 1, B + 1, B, TH, B, 2)[c]; z = rng.permutation(TH)
            if c in (1, 4, 6): z = np.concatenate([np.array([TH - 1]), z[z != TH - 1]])
            shut = z[n:]
            l = np.concatenate([np.array([z0]), p[1:T - 1:2]])
            d["a"][r, g, :TH] = 0; d["a"][r, g, shut] = 255
            d["nm"][r, g, 0, l[shut]] = p[2 * shut]; d["wt"][r, g, 0, l[shut]] = 255
    return pack(d)
def setup_inputs_crowd(rng):
    d, lab = parts(rng, 0.03, False)
    for g in range(4):
        c = rng.permutation(lab[g, int(rng.integers(0, NC))])[:4]
        x = d["nm"][:, g]; x[:, :, c] = c[rng.integers(0, 4, (N, 15, 4))]
        x = d["w15"][:, g]; x[:, c] = 255
        if g < 2: d["st"][:, g] = c[0]
        if g == 1: d["st"][np.arange(N), 1, rng.integers(0, T, N)] = c[1]
        if g == 2: d["st"][:, g] = c[rng.integers(0, 4, (N, T))]
        if g == 3: d["st"][:, g] = np.where(np.arange(T) % 2 == 0, c[0], c[1])
        for n in ("a", "b"): d[n][:, g] = rng.integers(0, 30, (N, RO * T)) * rng.integers(0, 2, (N, RO * T))
    d["v"][:, 0] = 255; d["v"][:, 1] = 0
    d["ob"][:, 7, :, 1::2] = 0
    tight(rng, d, 7, 0)
    return pack(d)
def setup_inputs_calm(rng):
    d, lab = parts(rng, 0.0, False)
    d["w15"][:] = 255; d["xb"][:] = 0; d["xb"][:, :, 0] = 15; d["ob"][:, :, 0] = 0
    for g in range(8):
        for par in range(2):
            pos = 1 + rng.permutation(15)[:g % 4]
            x = d["ob"][:, g, 0]; x[:, 2 * pos + par] = 15
            for w in range(RO):
                j = (2 * w + par) * TH + pos
                x = d["v"][:, g]; x[:, j] = 255
                x = d["a"][:, g]; x[:, j] = 0
    return pack(d)
def check_ranges(d):
    bad = []
    for k, lo, hi in (("lk", 1, 256 * H - 1), ("em", 0, 15), ("ob", 0, 15), ("xb", 0, 15), ("pe", 0, H - 1), ("po", 0, H - 1), ("nua", 0, 255), ("nub", 0, 255), ("vd", 0, 255)):
        x = np.asarray(d[k]).astype(np.float64)
        if not (np.min(x) >= lo and np.max(x) <= hi): bad.append("range of " + k)
        elif np.any(x != np.floor(x)): bad.append(k + " is not whole")
    x = np.asarray(d["lk"]).astype(np.int64)
    if np.any((x & 255) == 0): bad.append("a weight of lk is 0")
    if np.any(x.reshape(N, 8, 16, H)[:, :, 15] > 255): bad.append("a leftover of lk has a name")
    return bad
def pick(tab, ix):
    return np.take_along_axis(tab, ix.reshape(8, 1, -1), 2).reshape((8, 16) + ix.shape[1:])
def reference(lk, em, ob, xb, pe, po, nua, nub, vd):
    P = lk.astype(np.int64).reshape(N, 8, 16, H); E = em.astype(np.float32).astype(np.int64).reshape(N, 8, 16, H)
    O = ob.astype(np.float32).astype(np.int64).reshape(N, 8, 16, T); base = xb.astype(np.float32).astype(np.int64).reshape(N, 8, 16)
    st = np.zeros((N, 8, T), np.int64)
    for b in range(N): st[b, :, 0::2] = gentries(pe[b]); st[b, :, 1::2] = gentries(po[b])
    na = nua.astype(np.int64); nb = nub.astype(np.int64); vv = vd.astype(np.int64)
    named = (np.arange(16) < 15)[None, :, None]; acc = np.zeros((N, 8, 16, T), np.float64)
    for h in range(2 * RO):
        w, par = h >> 1, h & 1; cut = slice(h * TH, (h + 1) * TH)
        for r in range(N):
            b = (r + w) % N; path = st[b]
            if par == 0: s, q, l = path[:, 0::2], path[:, 1::2], np.concatenate([st[(b - 1) % N][:, T - 1:], path[:, 1:T - 1:2]], axis=1)
            else: s, l, q = path[:, 1::2], path[:, 0::2], np.concatenate([path[:, 2::2], st[(b + 1) % N][:, :1]], axis=1)
            y = O[b][:, :, par::2]; v = vv[r][:, cut]
            A = pick(P[r], l); nm, wt = A >> 8, A & 255
            u = (na[r][:, cut] * np.sum(np.where(named & (nm == s[:, None, :]), wt, 0), axis=1)) >> 8
            D = pick(P[r], s)
            u2 = (nb[r][:, cut] * np.sum(np.where(named & ((D >> 8) == q[:, None, :]), D & 255, 0), axis=1)) >> 8
            C = pick(P[r], nm)
            hold = np.any(named[..., None] & ((C >> 8) == q[:, None, None, :]) & ((C & 255) > u2[:, None, None, :]), axis=1)
            hold[:, 15] = True
            F = pick(E[r], nm); F[:, :, 15] = base[r][:, :, None]
            e = np.sum(F * y[:, :, None, :], axis=1)
            sv = (wt > u[:, None, :]) & hold
            c = np.add.accumulate(np.where(sv, e, 0), axis=1)
            hit = 256 * c > v[:, None, :] * c[:, 15:16]; got = hit[:, 15]; k = np.argmax(hit, axis=1)
            gw = np.where(sv, 1.0, 0.5) * np.exp(e * 2.0 ** -12)
            acc[r][:, :, par::2] = 0.5 * acc[r][:, :, par::2] + np.sum(gw[:, None] * F, axis=2)
            first = np.zeros((8, TH), bool)
            for g in range(8): first[g, np.unique(l[g], return_index=True)[1]] = True
            ask = (got & (k == 15) & first).astype(np.int64); before = np.add.accumulate(ask, axis=1) - ask; born = (ask == 1) & (before < B)
            ns = np.where(got & (k < 15), np.take_along_axis(nm, k[:, None, :], 1)[:, 0], s); ns = np.where(born, S + h * B + before, ns)
            for g in range(8):
                i = np.flatnonzero(first[g] & got[g] & (k[g] < 15)); ki = k[g, i]
                P[r, g, ki, l[g, i]] = 256 * nm[g, ki, i] + np.minimum(wt[g, ki, i] + 16, 255)
                i = np.flatnonzero(born[g]); j = before[g, i]; new = S + h * B + j
                P[r, g, j & 7, l[g, i]] = 256 * new + 128
                tile = A[g][:, i]; tile[0] = 256 * q[g, i] + 128
                P[r, g][:, new] = tile; E[r, g][:, new] = y[g][:, i]
            st[b, :, par::2] = ns
    z = np.zeros((N, 8, 16, T), np.float64)
    for r in range(N):
        A = pick(P[r], st[(r + RO - 1) % N]); F = pick(E[r], A >> 8); F[:, :, 15] = base[r][:, :, None]
        z[r] = np.sum((A & 255)[:, None] * F, axis=2)
    return {"ya": acc.reshape(N, 128, T).astype(np.float32), "yz": z.reshape(N, 128, T).astype(np.float32)}

def check_inputs(d):
    bad = list(check_ranges(d))
    if not bad:
        for name, y in reference(**d).items():
            for q in range(N):
                v = np.abs(np.asarray(y[q], np.float64)); s = np.sqrt(np.mean(v * v))
                if v.max() > 8 * s or s < 2.0 ** 4: bad.append('%s of rank %d is uneven or too small' % (name, q))
    return bad

import math
from concourse.bass import DstId, RemoteDMATransfer
from concourse.mybir import dt, AluOpType, AxisListType, ActivationFunctionType

ALU = AluOpType
ACT = ActivationFunctionType
H, S0, NB, TH, NSW = 3840, 3648, 32, 256, 3
PW = 4128
MAG = 193.0 * 256.0
M31 = 1.5 * 2.0 ** 31
BIG = 2.0 ** 22
LN2 = math.log(2.0)
WW = 328
NCH = 8
CW = H // NCH

F32, BF, I32, U16 = "float32", "bfloat16", "int32", "uint16"
SCRATCH = {}


def _buf(name, cols, dtype, where="sbuf"):
    SCRATCH[name] = (where, [128, cols], dtype)


for _n, _c, _d in [
    ("P", PW, F32), ("E", 3856, BF), ("lki", H, I32), ("tm0", CW, F32), ("tm1", CW, F32),
    ("Cw", 4096, F32), ("Fw0", 4096, BF), ("Fw1", 4096, BF), ("zz", 4096, BF), ("eq", 4096, BF), ("prod", 4096, BF),
    ("so", 4096, F32), ("Mq", 2432, BF),
    ("pin", 48, I32), ("abvi", 768, I32), ("abv", 768, BF), ("ob0", 512, BF), ("ob1", 512, BF), ("ob2", 512, BF),
    ("A0", WW, F32), ("A1", WW, F32), ("Ap", WW, F32), ("Bw", WW, F32), ("Y0", WW + 8, BF), ("Y1", WW + 8, BF),
    ("EVo", WW, F32), ("ODo", WW, F32), ("nf0", 288, BF), ("nf1", 288, BF),
    ("OD0", 264, F32), ("OD1", 264, F32), ("OD2", 264, F32), ("EV0", 256, F32), ("EV1", 256, F32), ("EV2", 256, F32),
    ("EC", 24, F32), ("LO0", 24, U16), ("LO1", 24, U16), ("LO2", 24, U16), ("LE", 48, U16),
    ("LEo", 16, U16), ("LOo", 16, U16),
    ("of0", 304, U16), ("of1", 304, U16), ("n0", 256, F32), ("n1", 256, F32), ("Lu", 256, U16), ("lf", 24, F32),
    ("dd", 512, BF), ("da", 512, BF), ("mm", 512, BF), ("ma", 512, F32), ("u2", 256, I32), ("sg", 256, BF),
    ("cap", 256, F32), ("ql", 256, F32), ("svB", 256, F32), ("svh", 256, F32), ("se", 256, F32), ("sev", 256, F32),
    ("xx", 256, F32), ("hit", 256, F32), ("hd", 256, F32), ("hf", 296, BF), ("cum", 296, F32), ("junk", 592, BF),
    ("cnt2", 2, F32), ("idx", 2, U16), ("t32", 32, F32), ("nb", 256, F32), ("sc", 256, F32),
    ("o1a", 48, F32), ("o1", 24, U16), ("tl", 1024, BF), ("R", 1024, BF),
    ("acc", 512, F32), ("oa", 512, F32), ("oz", 512, F32),
    ("ci", 4, I32), ("col", 24, F32), ("kc", 288, F32), ("bd", 544, F32), ("keepm", 256, F32), ("bdb", 256, BF),
    ("N0", 128, F32), ("SGh", 128, F32), ("thr", 288, F32), ("d1", 296, F32), ("mc", 192, F32), ("lnk", 192, F32), ("m8", 192, F32),
    ("k8", 32, F32), ("dum", 24, F32), ("ai", 40, I32), ("al", 40, U16), ("t16", 16, F32),
    ("one", 144, F32), ("SG", 128, F32), ("nSG", 128, F32), ("Idf", 128, F32), ("nId", 128, F32), ("Tri", 128, F32),
    ("nS17", 128, F32), ("Dn", 128, F32), ("E14", 128, F32), ("DA", 128, F32), ("DB", 128, F32), ("D15", 128, F32),
    ("rep", 128, F32), ("Z", 144, BF), ("Idb", 128, BF), ("Id8", 128, BF), ("Dif", 128, BF), ("ASK", 128, BF),
    ("POW", 128, BF), ("TWO", 128, BF), ("ZER", 128, BF), ("BC", 1024, BF), ("SEL", 768, BF), ("s256", 128, BF),
]:
    _buf(_n, _c, _d)
for _i in range(8):
    _buf("B%d" % _i, 512, F32, "psum")

NDMA = 56
SEMAPHORES = ["sv", "ss", "sp", "sgp"] + ["d%d" % i for i in range(NDMA)] + ["r%d" % i for i in range(20)]
ENGSEM = {"v": "sv", "s": "ss", "p": "sp", "g": "sgp"}


def rank_program(g, core, T, topo):
    rank = T.rank_of(core)
    if rank is None:
        return
    cores = list(T.cores)
    n = len(cores)
    Q = {"v": g.vector, "s": g.scalar, "p": g.tensor, "g": g, "y": g.sync}
    ops = []
    state = {"dma": 0}

    def a(name, c0=0, c1=None, step=1, p0=0, p1=128, ps=1):
        if c1 is None:
            c1 = SCRATCH[name][1][1]
        return ("a", name, c0, c1, step, p0, p1, ps)

    def ind(win, off):
        return ("i", win, off)

    def mk(x):
        if isinstance(x, tuple) and x[0] == "a":
            return T[x[1]][x[5]:x[6]:x[7], x[2]:x[3]:x[4]]
        if isinstance(x, tuple) and x[0] == "i":
            return mk(x[1]).indirect(mk(x[2]))
        return x

    def spans(xs):
        out = []
        for x in xs:
            if isinstance(x, tuple) and x[0] == "a":
                out.append((x[1], x[2], x[3]))
            elif isinstance(x, tuple) and x[0] == "i":
                out += spans([x[1], x[2]])
        return out

    def op(eng, fn, outs, ins, kind="c", cnt=1, sem=None):
        wr, rd = [], spans(ins)
        for o in outs:
            if isinstance(o, tuple) and o[0] == "i":
                wr += spans([o[1]])
                rd += spans([o[2]])
            else:
                wr += spans([o])
        ops.append({"eng": eng, "fn": fn, "wr": wr, "rd": rd, "kind": kind, "cnt": cnt, "sem": sem})

    def tt(o, x, y, alu):
        op("v", lambda: g.vector.tensor_tensor(mk(o), mk(x), mk(y), alu), [o], [x, y])

    def ts(o, x, s1, op0, s2=None, op1=None):
        if op1 is None:
            op("v", lambda: g.vector.tensor_scalar(mk(o), mk(x), mk(s1), None, op0), [o], [x, s1])
        else:
            op("v", lambda: g.vector.tensor_scalar(mk(o), mk(x), mk(s1), mk(s2), op0, op1), [o], [x, s1, s2])

    def cp(o, x):
        op("v", lambda: g.vector.tensor_copy(mk(o), mk(x)), [o], [x])

    def ms(o, val):
        op("v", lambda: g.vector.memset(mk(o), val), [o], [])

    def scan(o, d0, d1, op0, op1):
        op("v", lambda: g.vector.tensor_tensor_scan(mk(o), mk(d0), mk(d1), 0.0, op0, op1), [o], [d0, d1])

    def act(o, x, func=ACT.Identity, bias=0.0, scale=1.0, accum=None):
        if accum is None:
            op("s", lambda: g.scalar.activation(mk(o), mk(x), func, bias=mk(bias), scale=mk(scale)), [o], [x, bias, scale])
        else:
            op("s", lambda: g.scalar.activation(mk(o), mk(x), func, bias=mk(bias), scale=mk(scale), accum_out=mk(accum)),
               [o, accum], [x, bias, scale])

    def mm(o, l, r, start=True, stop=True):
        op("p", lambda: g.tensor.matmul(mk(o), mk(l), mk(r), start, stop), [o], [l, r])

    def iota(o, pattern, base, cm):
        if SCRATCH[o[1]][2] == I32:
            op("g", lambda: g.iota(mk(o), pattern, base, cm), [o], [])
        else:
            op("g", lambda: g.iota(mk(o), pattern, base, cm, allow_small_or_imprecise_dtypes=True), [o], [])

    def sel(o, x, pattern, cmp, fill, base, cm):
        op("g", lambda: g.affine_select(mk(o), mk(x), pattern, cmp, fill, base, cm), [o], [x])

    def newsem():
        state["dma"] += 1
        return "d%d" % (state["dma"] - 1)

    def dma(q, o, x, slow=False):
        if slow:
            op(q, lambda: Q[q].dma_start(mk(o), mk(x), allow_slow_non_contiguous=True), [o], [x], "d", 16, newsem())
        else:
            op(q, lambda: Q[q].dma_start(mk(o), mk(x)), [o], [x], "d", 16, newsem())

    def send(dst_rank, o, x, rsem):
        dst = cores[dst_rank % n]
        rid, pid = topo.addr(dst)[0], topo.addr(dst)[1]
        m = topo.mask(core, dst)
        ls = newsem()
        op("g", lambda: g.remote_dma(mk(o), mk(x), T.sem[rsem], T.sem[ls], pid, rid, m), [], [x], "r",
           len(topo.engines(core, dst)), ls)

    def landed(src_rank, o, rsem):
        op(None, None, [o], [], "l", len(topo.engines(cores[src_rank % n], core)), rsem)

    C = lambda j: a("col", j, j + 1)
    KR, G16, IS15, C15, NCOL, SVT, HITT, I15M, J0, J1, TB, RB, QB, POWC, AS, H0, P8 = range(17)
    grp = [[-16, 8], [0, 16]]

    dma("y", a("pin", 16, 32), T.po[:])
    dma("s", a("pin", 32, 48), T.pe[:])
    for c in range(NCH):
        dma("y" if c % 2 == 0 else "s", a("lki", c * CW, (c + 1) * CW), T.lk[:, c * CW:(c + 1) * CW])
    dma("y", a("E", 0, H), T.em[:])
    dma("y", a("ob0"), T.ob[:])
    for j, t in enumerate((T.nua, T.nub, T.vd)):
        dma("y", a("abvi", j * 256, (j + 1) * 256, p1=48), t[:])
    iota(a("ci", 0, 1), [[0, 1]], 0, 1)
    iota(a("kc"), [[0, 18], [1, 16]], 0, 0)
    iota(a("ai"), [[1, 40]], 0, 0)

    ms(a("one"), 1.0)
    sel(a("SG"), a("one", 0, 128), grp, ALU.is_ge, 0.0, 0, 1)
    sel(a("SG"), a("SG"), [[16, 8], [0, 16]], ALU.is_ge, 0.0, 15, -1)
    sel(a("Idf"), a("one", 0, 128), [[-1, 128]], ALU.is_equal, 0.0, 0, 1)
    send(rank + 1, a("pin", 0, 16), a("pin", 16, 32), "r0")
    landed(rank - 1, a("pin", 0, 16), "r0")
    dma("g", a("E", H, H + 1), T.xb[:], slow=True)
    ms(a("s256"), 1.0 / 256)
    ms(a("P", H, PW), 0.0)
    ts(a("ci", 1, 2), a("ci", 0, 1), 15, ALU.bitwise_and)
    ts(a("ci", 2, 3), a("ci", 0, 1), 112, ALU.bitwise_and)
    ts(a("ci", 3, 4), a("ci", 0, 1), 7, ALU.bitwise_and)
    ms(a("ZER"), 0.0)
    cp(a("col", KR, G16 + 1), a("ci", 1, 3))
    cp(C(P8), a("ci", 3, 4))
    ms(a("hf"), 0.0)
    ts(C(IS15), C(KR), 15.0, ALU.is_equal)
    ts(C(C15), C(KR), 15.0, ALU.is_equal, float(H), ALU.mult)
    ts(C(NCOL), C(KR), 15.0, ALU.is_equal, -512.0 * H, ALU.mult)
    ts(C(J0), C(KR), 0.5, ALU.add)
    ts(C(J1), C(KR), 16.5, ALU.add)
    ts(C(TB), C(KR), 8.0, ALU.is_lt, -200.0, ALU.mult)
    ts(C(AS), C(KR), 14.0, ALU.is_equal, -1.0, ALU.mult)
    ts(C(H0), C(KR), 0.0, ALU.is_equal, 0.5, ALU.mult)
    ts(C(SVT), C(IS15), -1.0, ALU.mult, 8.5, ALU.add)
    ts(C(HITT), C(IS15), -2.0 ** -26, ALU.add)
    ts(C(I15M), C(IS15), -1.0, ALU.add)
    ts(C(RB), C(IS15), -2000.0, ALU.mult, 256.0, ALU.add)
    ts(C(QB), C(IS15), 2.0 ** 21, ALU.mult, 128.0 - MAG, ALU.add)
    tt(C(AS), C(AS), C(IS15), ALU.add)
    ms(a("DA"), 0.0)
    ms(a("DB"), 0.0)
    ms(a("B0", 0, 512, 16), 0.0)
    ms(a("B1", 0, 512, 16), 0.0)

    for nm in ("A0", "A1", "Ap", "Bw", "EVo", "ODo"):
        act(a(nm, 0, 40), a("one", 0, 40), scale=0.0)
        act(a(nm, 280, WW), a("one", 0, WW - 280), scale=0.0)
    for nm in ("Y0", "Y1"):
        act(a(nm, 0, 32), a("one", 0, 32), scale=0.0)
        act(a(nm, 280, WW + 8), a("one", 0, WW + 8 - 280), scale=0.0)
    act(a("nf0", 0, 32), a("one", 0, 32))
    act(a("nf0", 280, 288), a("one", 0, 8))
    for c in range(2):
        act(a("d1", c * 128, c * 128 + 128), a("one", 0, 128), scale=0.0)
        act(a("nb", c * 128, c * 128 + 128), a("one", 0, 128), scale=0.5)

    sel(a("SEL", 0, 128, p1=48), a("s256", p1=48), [[-6, 8], [0, 16]], ALU.is_equal, 0.0, 0, 1)
    iota(a("cum", 0, 144), [[1, 144]], -15, 0)
    iota(a("dum"), [[16, 24]], H + 1, 0)
    sel(a("Dn"), a("Idf"), [[-1, 128]], ALU.not_equal, -1.0, -1, 1)
    sel(a("Dn"), a("Dn"), grp, ALU.not_equal, 0.0, -16, 1)
    sel(a("Tri"), a("SG"), [[1, 128]], ALU.is_ge, 0.0, 0, -1)
    iota(a("mc"), [[512, 192]], 512 * S0, 0)
    iota(a("m8"), [[0, 24], [1, 8]], 0, 0)
    iota(a("d1", 256, 296), [[1, 40]], 0, 0)
    sel(a("Dif"), a("ZER"), [[-1, 128]], ALU.not_equal, 16.0, 0, 1)
    sel(a("Dif"), a("Dif"), [[-1, 128]], ALU.not_equal, -16.0, 1, 1)
    sel(a("Dif"), a("Dif"), [[0, 8], [1, 16]], ALU.not_equal, 0.0, -15, 0)
    sel(a("Dif"), a("Dif"), grp, ALU.is_ge, 0.0, 0, 1)
    dstep = [[-16, 8], [0, 2], [-1, 8]]
    for nm, off in (("DA", 0), ("DB", -8)):
        sel(a(nm), a(nm), dstep, ALU.not_equal, -1.0, off, 1)
        sel(a(nm), a(nm), dstep, ALU.not_equal, 1.0, off + 1, 1)
    sel(a("DA"), a("DA"), grp, ALU.is_ge, 0.0, 0, 1)
    send(rank - 1, a("ob1"), a("ob0"), "r1")
    send(rank - 2, a("ob2"), a("ob0"), "r2")
    landed(rank + 1, a("ob1"), "r1")
    landed(rank + 2, a("ob2"), "r2")
    for h in range(1, 6):
        sel(a("SEL", h * 128, (h + 1) * 128, p1=48), a("s256", p1=48), [[-6, 8], [0, 16]], ALU.is_equal, 0.0, -h, 1)

    def conv1(c):
        ts(a("tm%d" % (c % 2)), a("lki", c * CW, (c + 1) * CW), -128.0, ALU.add, M31, ALU.add)
        act(a("B%d" % (2 + c % 4), 0, CW), a("tm%d" % (c % 2)), bias=-M31)

    def conv2(c):
        tt(a("P", c * CW, (c + 1) * CW), a("B%d" % (2 + c % 4), 0, CW), a("lki", c * CW, (c + 1) * CW), ALU.add)

    def mats0():
        for c in range(2):
            ts(a("bd", c * 272, (c + 1) * 272), a("kc", 0, 272), C(KR), ALU.is_equal, BIG, ALU.mult)
        cp(a("al"), a("ai"))

    smats = [("rep", "SG", 512.0 / BIG), ("TWO", "SG", 2.0), ("Idb", "Idf", 1.0), ("nSG", "SG", -1.0), ("nId", "Idf", -1.0),
             ("Id8", "Idf", 8.0), ("nS17", "SG", -2.0 ** -17), ("ASK", "SG", C(AS)), ("D15", "SG", C(IS15)),
             ("N0", "SG", C(H0)), ("SGh", "SG", 0.5)]

    def mats1():
        ts(a("sev"), a("kc", 0, 256), 0.0, ALU.is_equal, 2.0, ALU.mult)
        cp(a("abv", p1=48), a("abvi", p1=48))
        scan(a("thr", 0, 256), a("nb"), a("sev"), ALU.mult, ALU.max)
        ts(a("Z"), a("cum", 0, 144), C(G16), ALU.is_equal)
        tt(a("t16"), a("thr", 0, 16), a("bd", 0, 16), ALU.mult)
        cp(a("thr", 256, 288), a("thr", 0, 32))
        op("v", lambda: g.vector.tensor_reduce(mk(C(POWC)), mk(a("t16")), AxisListType.X, ALU.add), [C(POWC)], [a("t16")])
        ts(a("dum"), a("dum"), C(KR), ALU.add, 1.0 / 16, ALU.mult)
        ts(a("POW"), a("SG"), C(POWC), ALU.mult, 0.5 / BIG, ALU.mult)
        ts(a("keepm"), a("kc", 0, 256), 0.0, ALU.not_equal)
        ts(a("t16", 0, 8), a("kc", 0, 8), C(P8), ALU.is_equal)
        ts(a("m8"), a("m8"), C(KR), ALU.is_equal)
        ts(a("lnk"), a("mc"), 128.0, ALU.add)
        ts(a("k8"), a("m8", 0, 32), -1.0, ALU.mult, 1.0, ALU.add)
        tt(a("lnk"), a("lnk"), a("m8"), ALU.mult)

    def mats2():
        act(a("E14"), a("Dn"), scale=C(IS15))
        act(a("bdb"), a("bd", 0, 256))
        act(a("Tri"), a("Tri"), scale=2.0 ** -17)

    def mats3():
        for kk in range(8):
            act(a("BC", kk * 128, (kk + 1) * 128), a("SG"), scale=a("t16", kk, kk + 1))

    conv1(0)
    for c in range(NCH):
        if c + 1 < NCH:
            conv1(c + 1)
        conv2(c)
        if c == 0:
            mats0()
        for nm, src, sca in smats[2 * c - 2:2 * c] if c > 0 else []:
            act(a(nm), a(src), scale=sca)
        if c == 5:
            cp(a("LO0", 6, 24), a("pin", 14, 32))
            cp(a("LE", 0, 16), a("pin", 32, 48))
            tt(a("so", 0, 544), ind(a("pin", 8, 48), a("al", 6, 40)), a("bd", 0, 544), ALU.mult)
            mm(a("B6", 0, 272), a("rep"), a("so", 16, 288))
            mm(a("B7", 0, 256), a("rep"), a("so", 288, 544))
    act(a("OD0", 7, 264), a("B6", 15, 272))
    act(a("EV0"), a("B7", 0, 256))

    RED = lambda k: a("Z", 15 - k, 143 - k)

    def acc_prep_pe(x=a("xx"), b="B7"):
        mm(a(b, 0, 256), a("DA"), x)
        mm(a(b, 256, 512), a("DB"), x)

    def acc_prep_s(scale, b="B7", o=0):
        act(a("tl", o, o + 512), a(b), ACT.Exp, bias=C(TB), scale=scale)
        act(a(b), a(b), ACT.Exp, scale=scale)

    def acc_prep_v(b="B7", o=0, ro=0):
        tt(a("R", ro, ro + 512), a(b), a("tl", o, o + 512), ALU.subtract)

    def bc(c, ro=0):
        b = "B%d" % (c % 2)
        for k in range(1, 16):
            o = ro + (k // 8) * 256 + c * 32
            mm(a(b, k, 512, 16), a("BC", (k % 8) * 128, (k % 8 + 1) * 128), a("R", o, o + 32))

    def sc(c, F):
        scan(a("so", c * 512, (c + 1) * 512), a("B%d" % (c % 2)), a(F, c * 512, (c + 1) * 512), ALU.mult, ALU.add)

    def acc_end(kind, par, gg=a("B2", 256, 512)):
        s15 = a("so", 15, 4096, 16)
        ac = a("acc", par * 256, (par + 1) * 256)
        if kind == 0:
            tt(ac, gg, s15, ALU.mult)
        elif kind == "z":
            tt(a("oz", par, 512, 2), gg, s15, ALU.mult)
        else:
            tt(gg, gg, s15, ALU.mult)
            tt(ac if kind == 1 else a("oa", par, 512, 2), gg, ac, ALU.add)

    def half(h):
        w, par = h // 2, h % 2
        A, NN, OF, F, Y, NF = ("%s%d" % (x, par) for x in ("A", "n", "of", "Fw", "Y", "nf"))
        ob = a("ob%d" % w, par, 512, 2)
        m0 = S0 + NB * h
        if par == 0:
            base, na = 31, 17
            ll, ls = a("LO%d" % w, 6, 24), a("LE", 16 * w, 16 * w + 16)
            l, q, s = a("OD%d" % w, 7, 263), a("OD%d" % w, 8, 264), a("EV%d" % w)
            ga, go, NS, LN = a(A, 0, 288), a(OF, 1, 289), "EVo", "LEo"
        else:
            base, na = 32, 16
            ll, ls = a("LEo"), a("LO%d" % w, 8, 24)
            l, q, s = a("EVo", 31, 287), a("EVo", 32, 288), a("OD%d" % w, 8, 264)
            ga, go, NS, LN = a(A, 32, 288), a(OF, 32, 288), "ODo", "LOo"
        As = a(A, base, base + 256)
        offs = lambda c0, c1: a(OF, 32 + c0, 32 + c1)
        Pw, Ew = a("P"), a("E", 0, H + 1)

        PF = "Fw%d" % (1 - par)
        todo = list(range(8)) if h > 0 else []

        def psc():
            if todo:
                c = todo.pop(0)
                sc(c, PF)
                if c + 2 < 8:
                    bc(c + 2)

        def acc_turn():
            if h > 0:
                acc_prep_v()
                bc(0)
                bc(1)
            if h > 1:
                acc_end((h - 2) // 2, par)

        if par == 0:
            acc_turn()
        ts(go, ind(Pw, ll), 1.0 / 512, ALU.mult, C(C15), ALU.add)
        act(ga, ind(Pw, ll))
        act(a(F), ind(Ew, offs(0, 256)))
        if par == 1:
            acc_turn()
        if h > 0:
            mm(a("B2", 256, 512), a("D15"), a("xx"))
        if h == 0:
            mats1()
        dma("y", a(Y, base + 257, base + 289), T.em[:, m0:m0 + NB])
        dma("y", a("Bw", base, base + 256), As)
        sl = a("SEL", h * 128, (h + 1) * 128, p1=48)
        mm(a("B5"), sl, a("abv", 0, 512, p1=48))
        mm(a("B3", 256, 512), sl, a("abv", 512, 768, p1=48))

        mm(a("B6", 256, 512), a("Idb"), ob)

        def firsts(between):
            ts(a("Lu"), l, 1.0 / 512, ALU.mult)
            if par == 0:
                ts(a("lf", 0, 1), a("LO%d" % w, 7, 8), C(IS15), ALU.mult, C(I15M), ALU.add)
                cp(a("lf", 1, 17), a("LO%d" % w, 8, 24))
            else:
                cp(a("lf", 0, 16), ll)
            sh = 15 if par == 0 else 0
            mm(a("B6", 0, 256), a("ZER"), a("hf", 0, 256), True, False)
            pos = 0
            for j in range(na):
                c0, c1 = max(0, 16 * j - sh), min(256, 16 * j + 16 - sh)
                ts(a("Mq", pos, pos + 256 - c0), a("Lu", c0, 256), a("lf", j, j + 1), ALU.is_equal)
                mm(a("B6", c0, c1), a("POW"), a("Mq", pos, pos + c1 - c0), False, c1 == 256)
                if c1 < 256:
                    mm(a("B6", c1, 256), a("TWO"), a("Mq", pos + c1 - c0, pos + 256 - c0), False, False)
                pos += 256 - c0
                if j in between:
                    psc()
            return sh

        def slices():
            tt(a("dd", 0, 256), As, s, ALU.subtract)
            tt(a("dd", 256, 512), ind(Pw, ls), q, ALU.subtract)
            act(a("da"), a("dd"), ACT.Abs, bias=-256.0)
            act(a("mm"), a("da"), ACT.Relu, bias=C(RB), scale=-1.0)
            act(a("B7", 0, 256), q, bias=C(QB))

        if par == 0:
            for _ in range(3):
                psc()
            slices()
            sh = firsts((3, 9))
        else:
            psc()
            psc()
            cp(a("EVo", 287, 288), a("EC", 8 * w, 8 * w + 1))
            psc()
            slices()
            sh = firsts((3, 9))
        if h > 0:
            act(a("B2", 256, 512), a("B2", 256, 512), ACT.Exp, bias=math.log(0.5 ** (NSW - (h - 1) // 2)), scale=1.0 / 4096)
        act(a("Cw", 0, 2048), ind(Pw, offs(0, 128)))
        act(a("ql"), As, bias=2 * M31)
        act(a(NN), a("ql"), bias=-2 * M31)
        if h == 0:
            mats2()
        tt(a(NF, base, base + 256), a("B6", 0, 256), a("thr", sh, sh + 256), ALU.is_ge)
        d0 = 32 - 16 * (na - 16)

        def prods(k0, k1):
            for k in range(k0, k1):
                tt(a("prod", k * 256, (k + 1) * 256), a("B6", 256, 512), a(F, k, 4096, 16), ALU.mult)
                mm(a("B3", 0, 256), RED(k), a("prod", k * 256, (k + 1) * 256), k == 0, k == 15)

        act(a("Cw", 2048, 4096), ind(Pw, offs(128, 256)))
        for b in range(16):
            mm(a("B2", 0, na), RED(b), a(NF, d0 + b, 288, 16), b == 0, b == 15)
        prods(0, 6)
        tt(a("o1a", 0, na), a("B2", 0, na), a("dum", 0, na), ALU.mult)
        prods(6, 8)
        tt(a("ma"), a("B5"), a("mm"), ALU.mult)
        mm(a("B5", 256, 512), a("SG"), a("ma", 256, 512))
        tt(a("o1a", 24, 24 + na), a("o1a", 0, na), a("lf", 0, na), ALU.max)
        prods(8, 12)
        ts(a("u2"), a("B5", 256, 512), 255.0, ALU.min, -0.498, ALU.add)
        cp(a("o1", 0, na), a("o1a", 24, 24 + na))
        prods(12, 16)
        mm(a("B5", 0, 256), a("Idf"), As, True, False)
        mm(a("B5", 0, 256), a("nId"), a(NN), False, False)
        mm(a("B5", 0, 256), a("nSG"), a("ma", 0, 256), False, True)
        tt(a("B7", 0, 256), a("B7", 0, 256), a("u2"), ALU.add)
        mm(a("B6", 256, 512), a("Dn"), a(NN), True, False)
        mm(a("B6", 256, 512), a("E14"), s, False, True)
        mm(a("B6", 0, 256), a("Idb"), a("bdb"))
        mm(a("B2", 0, 256), a("Idf"), As, True, False)
        act(a("sg"), a("B5", 0, 256), ACT.Sign, bias=-1.0 / 512)
        act(a("ql"), q, bias=128.0)
        dma("y", a("Bw", base, base + 256, ps=16), a("ql", ps=16))
        act(a("cap"), a(NN), bias=255.0)
        act(a(Y, base, base + 256), ob)
        if h == 0:
            mats3()
        mm(a("B4", 0, 256), a("Id8"), a("sg"), True, False)
        for hh in range(2):
            for k in range(16):
                o = hh * 2048 + k * 128
                tt(a("zz", o, o + 128), a("B7", hh * 128, 128 + hh * 128), a("Cw", hh * 2048 + k, (hh + 1) * 2048, 16),
                   ALU.subtract)
            for u in range(2):
                o = hh * 2048 + u * 1024
                ts(a("eq", o, o + 1024), a("zz", o, o + 1024), -MAG, ALU.is_equal)
                for k in range(8 * u, 8 * u + 8):
                    o = hh * 2048 + k * 128
                    mm(a("B4", hh * 128, hh * 128 + 128), RED(k), a("eq", o, o + 128), False, hh == 1 and k == 15)
        psc()
        ts(a("svB"), a("B4", 0, 256), C(SVT), ALU.is_gt, 8192.0 * LN2, ALU.mult)
        tt(a("se"), a("B3", 0, 256), a("svB"), ALU.min)
        act(a("svh"), a("svB"), scale=0.5)
        mm(a("B4", 256, 512), a("Tri"), a("se"), True, False)
        tt(a("sev"), a("B3", 256, 512), a("se"), ALU.mult)
        mm(a("B4", 256, 512), a("nS17"), a("sev"), False, True)
        tt(a("xx"), a("B3", 0, 256), a("svh"), ALU.add)
        mm(a("B3", 0, 256), a("N0"), a(NN), True, False)
        psc()
        tt(a("hf", 0, 256), a("B4", 256, 512), a(NF, base, base + 256), ALU.is_gt)
        mm(a("B5", 0, 289), a("ASK"), a("hf", 0, 289))
        act(a("hit"), a("B4", 256, 512), ACT.Sign, bias=C(HITT))
        mm(a("B2", 0, 256), a("Dif"), a("hf", 0, 256), False, True)
        scan(a("cum", 0, 289), a("B5", 0, 289), a("d1", 0, 289), ALU.add, ALU.max)
        tt(a("hd"), a("B6", 256, 512), a("hit"), ALU.mult)
        mm(a("B3", 0, 256), a("SGh"), a("hd"), False, True)
        acc_prep_pe()
        act(a("junk", 0, 289), a("cum", 0, 289), ACT.Sign, bias=C(J0), scale=-1.0, accum=a("cnt2", 0, 1))
        act(a("junk", 296, 585), a("cum", 0, 289), ACT.Sign, bias=C(J1), scale=-1.0, accum=a("cnt2", 1, 2))
        act(a(NS, base, base + 256), a("B3", 0, 256))
        tt(a("Ap", base, base + 256), a("B2", 0, 256), a("cap"), ALU.min)
        psc()
        ts(a("idx"), a("cnt2"), 0.5, ALU.mult, 144.5 + base, ALU.add)
        acc_prep_s(1.0 / 4096)
        ix = a("idx")
        cp(ind(a(NS), ix), a("mc", NB * h, NB * h + NB))
        tt(a("t32"), ind(a(A), ix), a("k8"), ALU.mult)
        if par == 0:
            send(rank - 1, a("EC", 8 * w, 8 * w + 8), a(NS, base, base + 8), "r%d" % (3 + w))
            landed(rank + 1, a("EC", 8 * w, 8 * w + 8), "r%d" % (3 + w))

        def lists():
            tt(a("nb"), a("B6", 0, 256), a(NS, base, base + 256), ALU.add)
            scan(a("sc"), a("keepm"), a("nb"), ALU.mult, ALU.max)
            ts(a(LN), a("sc", 15, 256, 16), -BIG, ALU.add, 1.0 / 512, ALU.mult)

        def edits():
            tt(ind(a("Ap"), ix), a("t32"), a("lnk", NB * h, NB * h + NB), ALU.add)
            cp(ind(Pw, a("o1", 0, na)), a("Ap", d0, 288))
            cp(a("Bw", base + 257, base + 289), a("P", m0, m0 + NB))
            cp(a("P", m0, m0 + NB), ind(a("Bw"), ix))

        lists()
        if w < NSW - 1:
            if par == 1:
                send(rank - 1, a("LO%d" % (w + 1), 8, 24), a(LN), "r%d" % (6 + w))
                send(rank - 1, a("OD%d" % (w + 1), 8, 264), a(NS, base, base + 256), "r%d" % (8 + w))
                landed(rank + 1, a("LO%d" % (w + 1), 8, 24), "r%d" % (6 + w))
                landed(rank + 1, a("OD%d" % (w + 1), 8, 264), "r%d" % (8 + w))
                cp(a("LO%d" % (w + 1), 6, 8), a(LN, 14, 16))
                act(a("OD%d" % (w + 1), 7, 8), a(NS, base + 255, base + 256))
            else:
                send(rank - 1, a("LE", 16 * w + 16, 16 * w + 32), a(LN), "r%d" % (10 + w))
                send(rank - 1, a("EV%d" % (w + 1)), a(NS, base, base + 256), "r%d" % (12 + w))
                landed(rank + 1, a("LE", 16 * w + 16, 16 * w + 32), "r%d" % (10 + w))
                landed(rank + 1, a("EV%d" % (w + 1)), "r%d" % (12 + w))
        act(a("E", m0, m0 + NB), ind(a(Y), ix))
        edits()

    for h in range(2 * NSW):
        half(h)

    Pw, Ew = a("P"), a("E", 0, H + 1)
    for par, ln in ((0, "LEo"), (1, "LOo")):
        ts(a("of%d" % par, 32, 288), ind(Pw, a(ln)), 1.0 / 512, ALU.mult, C(C15), ALU.add)
    act(a("Fw0", 0, 1024), ind(Ew, a("of0", 32, 96)))
    for par in range(2):
        ts(a("n%d" % par), a("of%d" % par, 32, 288), 512.0, ALU.mult, C(NCOL), ALU.add)
    for par, ln in ((0, "LEo"), (1, "LOo")):
        tt(a("oz", par * 256, par * 256 + 256), ind(Pw, a(ln)), a("n%d" % par), ALU.subtract)
    act(a("ma"), a("oz"), ACT.Ln)
    acc_prep_v()
    bc(0)
    bc(1)
    acc_end(2, 0)
    act(a("Fw0", 1024, 2048), ind(Ew, a("of0", 96, 160)))
    for c in range(8):
        sc(c, "Fw1")
        if c + 2 < 8:
            bc(c + 2)
        if c == 0:
            acc_prep_pe(a("ma", 0, 256), "B7")
        if c == 2:
            mm(a("B2", 256, 512), a("D15"), a("xx"))
        if c == 4:
            acc_prep_pe(a("ma", 256, 512), "B5")
        if c == 6:
            mm(a("B4"), a("D15"), a("oz"))
    acc_prep_s(1.0, "B7", 0)
    act(a("B2", 256, 512), a("B2", 256, 512), ACT.Exp, bias=math.log(0.5), scale=1.0 / 4096)
    act(a("Fw0", 2048, 3072), ind(Ew, a("of0", 160, 224)))
    act(a("Fw0", 3072, 4096), ind(Ew, a("of0", 224, 288)))
    acc_prep_s(1.0, "B5", 512)
    for c in range(4):
        act(a("zz", c * 1024, c * 1024 + 1024), ind(Ew, a("of1", 32 + 64 * c, 96 + 64 * c)))
    acc_prep_v("B7", 0, 512)
    bc(0, 512)
    bc(1, 512)
    acc_end(2, 1)
    dma("y", T.ya[:], a("oa"))
    for c in range(8):
        sc(c, "Fw0")
        if c == 5:
            acc_prep_v("B5", 512, 0)
        bc((c + 2) % 8, 512 if c + 2 < 8 else 0)
    acc_end("z", 0, a("B4", 0, 256))
    for c in range(8):
        sc(c, "zz")
        if c + 2 < 8:
            bc(c + 2)
    acc_end("z", 1, a("B4", 256, 512))
    dma("y", T.yz[:], a("oz"))

    acc = {}
    deps = []
    for i, o in enumerate(ops):
        d = set()
        for sp, isw in [(x, False) for x in o["rd"]] + [(x, True) for x in o["wr"]]:
            name, c0, c1 = sp
            ps = SCRATCH[name][0] == "psum"
            for (j, b0, b1, jw) in acc.get(name, []):
                pj = ops[j]
                same = pj["eng"] == o["eng"] and pj["kind"] == "c" and o["kind"] == "c"
                if ps and not same:
                    d.add(j)
                elif b0 < c1 and c0 < b1 and (isw or jw):
                    if not same or o["eng"] != "p":
                        d.add(j)
        for sp, isw in [(x, False) for x in o["rd"]] + [(x, True) for x in o["wr"]]:
            name, c0, c1 = sp
            lst = acc.setdefault(name, [])
            if isw:
                lst[:] = [e for e in lst if not (c0 <= e[1] and e[2] <= c1 and e[0] in d)]
            lst.append((i, c0, c1, isw))
            if len(lst) > 400:
                del lst[:100]
        d.discard(i)
        deps.append(d)
    order = {}
    for i, o in enumerate(ops):
        if o["kind"] == "c":
            o["seq"] = order.get(o["eng"], 0) + 1
            order[o["eng"]] = o["seq"]
    clock = {q: {} for q in Q}
    waits = []
    last = {}
    for i, o in enumerate(ops):
        ws = []
        if o["eng"] is not None:
            ck = clock[o["eng"]]
            for j in sorted(deps[i], reverse=True):
                pj = ops[j]
                key, val = (pj["eng"], pj["seq"]) if pj["kind"] == "c" else (pj["sem"], 1)
                if ck.get(key, 0) >= val:
                    continue
                ws.append(j)
                pj["need"] = True
                ck[key] = val
                for k2, v2 in pj["ck"].items():
                    if ck.get(k2, 0) < v2:
                        ck[k2] = v2
            o["ck"] = dict(ck)
            if o["kind"] == "c":
                last[o["eng"]] = i
        else:
            o["ck"] = {}
        waits.append(ws)
    count = {}
    for i, o in enumerate(ops):
        if o["eng"] is None:
            continue
        for j in waits[i]:
            pj = ops[j]
            if pj["kind"] == "c":
                Q[o["eng"]].wait_ge(T.sem[ENGSEM[pj["eng"]]], pj["val"])
            else:
                Q[o["eng"]].wait_ge(T.sem[pj["sem"]], pj["cnt"])
        ins = o["fn"]()
        if o["kind"] == "d":
            ins.then_inc(T.sem[o["sem"]], 16)
        elif o["kind"] == "c" and o.get("need"):
            count[o["eng"]] = count.get(o["eng"], 0) + 1
            o["val"] = count[o["eng"]]
            ins.then_inc(T.sem[ENGSEM[o["eng"]]], 1)
    for o in ops:
        if o["kind"] != "c" and not o.get("need"):
            g.wait_ge(T.sem[o["sem"]], o["cnt"])
